import numpy as np
import ml_dtypes


def mxq(x, axis, fmt="e4m3"):
    dtype, down = {"e4m3": (ml_dtypes.float8_e4m3fn, 7), "e5m2": (ml_dtypes.float8_e5m2, 14)}[fmt]
    v = np.moveaxis(np.asarray(x, np.float32).astype(ml_dtypes.bfloat16).astype(np.float64), axis, -1)
    blocks = v.reshape(v.shape[:-1] + (-1, 32))
    amax = np.abs(blocks).max(-1, keepdims=True)
    byte = np.maximum(np.where(amax > 0, np.frexp(amax)[1] - 1 + 127, 0) - down, 1)
    scale = np.exp2(byte - 127.0)
    codes = (blocks / scale).astype(np.float32).astype(dtype).astype(np.float64)
    return np.moveaxis((codes * scale).reshape(v.shape), -1, axis)


WIDE = False


def mx_kscale(k):
    if not WIDE:
        return np.ones(k)
    levels = np.array([10, -10, 5, -5, 0])
    if k % 512:
        return np.exp2(np.random.permutation(np.resize(levels, k // 32))).repeat(32)
    a = np.empty((k // 512, 16))
    for p in range(k // 512):
        a[p, :8] = np.random.permutation(np.resize(levels, 8))
        for g in range(8):
            far = levels[np.abs(levels - a[p, g]) >= 10]
            a[p, g + 8] = far[np.random.randint(len(far))]
    return np.exp2(a.ravel()).repeat(32)


def f64(x):
    return np.asarray(x).astype(np.float64)


def striped(idx):
    return np.tile(idx.reshape(-1, 16).T, (8, 1)).astype(np.uint16)


def unstriped(offs):
    return offs[:16].T.reshape(-1).astype(np.int64)


def striped8(idx):
    return np.concatenate([x.reshape(-1, 16).T for x in idx]).astype(np.uint16)


def runs(offs, k):
    lists = np.stack([offs[16 * r : 16 * r + 16].T.reshape(-1) for r in range(8)]).astype(np.int64)
    return lists[np.arange(k) % 512 // 64]


def pack_weight(w):
    k, n = w.shape
    w = f64(np.asarray(w, np.float32).astype(ml_dtypes.bfloat16)).reshape(k // 32, 32, n)
    amax = np.abs(w).max(1)
    byte = np.clip(np.where(amax > 0, np.frexp(amax)[1] - 1 + 127 - 7, 1), 1, 254)
    scaled = (w * np.exp2(127.0 - byte)[:, None, :]).reshape(k, n).astype(np.float32)
    words = np.ascontiguousarray(scaled.reshape(k // 512, 128, 4, n).transpose(0, 1, 3, 2)).astype(ml_dtypes.float8_e4m3fn).view(np.uint8)
    return words, np.ascontiguousarray(byte.astype(np.uint8).reshape(k // 512, 16, n))


def unpack_weight(words, scales):
    g, p, n, _ = words.shape
    vals = np.ascontiguousarray(words).view(ml_dtypes.float8_e4m3fn).astype(np.float64) * np.repeat(np.exp2(scales.astype(np.float64) - 127.0), 8, axis=1)[..., None]
    return vals.transpose(0, 1, 3, 2).reshape(g * 512, n)


def sigmoid(v):
    return 1.0 / (1.0 + np.exp(-np.maximum(v, -700.0)))

def planes(y):
    n, m = y.shape
    v = y.astype(np.float32).astype(ml_dtypes.bfloat16).astype(np.float64).reshape(n // 32, 32, m)
    top = np.abs(v).max(1)
    byte = np.clip(np.where(top > 0, np.frexp(top)[1] - 1 + 127 - 7, 1), 1, 254)
    codes = (v * np.exp2(127.0 - byte)[:, None, :]).reshape(n, m).astype(np.float32).astype(ml_dtypes.float8_e4m3fn).view(np.uint8)
    words = codes.reshape(n // 512, 128, 4, m).transpose(0, 1, 3, 2)
    return np.ascontiguousarray(words), np.ascontiguousarray(byte.astype(np.uint8).reshape(n // 512, 16, m))


K, T, S, N, H = 512, 2048, 256, 512, 512


def setup_inputs():
    n = np.random.standard_normal
    s = mx_kscale(K)[:, None]
    u = mx_kscale(H)
    packed_xT = pack_weight(n((K, T)) * s)
    packed_w1 = pack_weight(n((K, H)) / np.sqrt(K) / s)
    packed_w2 = pack_weight(n((K, H)) / np.sqrt(K) / s)
    packed_w3 = pack_weight(n((H, N)) / np.sqrt(2 * H) / u[:, None])
    packed_w4 = pack_weight(n((H, N)) / np.sqrt(2 * H) / u[:, None])
    return {
        "x_words": packed_xT[0],
        "x_scales": packed_xT[1],
        "w1_words": packed_w1[0],
        "w1_scales": packed_w1[1],
        "w2_words": packed_w2[0],
        "w2_scales": packed_w2[1],
        "tau": np.random.uniform(0.3, 0.9, (H, 1)).astype(np.float32),
        "sl": np.random.uniform(1.0, 2.0, (H, 1)).astype(np.float32),
        "th": (0.5 * n((H, 1))).astype(np.float32),
        "gn": (np.random.uniform(0.5, 1.5, (H, 1)) * u[:, None]).astype(np.float32),
        "gm": (np.random.uniform(0.5, 1.5, (H, 1)) * u[:, None]).astype(np.float32),
        "w3_words": packed_w3[0],
        "w3_scales": packed_w3[1],
        "w4_words": packed_w4[0],
        "w4_scales": packed_w4[1],
        "offs": striped(np.random.permutation(T)[:S]),
        "hz": striped8(np.random.randint(0, T, (8, S))),
        "n1": striped8(np.stack([np.random.permutation(S) for _ in range(8)])),
        "n2": striped(np.random.permutation(S)),
        "n3": striped(np.random.permutation(S)),
        "n4": striped8(np.stack([np.random.permutation(S) for _ in range(8)])),
        "n5": striped8(np.stack([np.random.permutation(S) for _ in range(8)])),
    }


def reference(x_words, x_scales, w1_words, w1_scales, w2_words, w2_scales, tau, sl, th, gn, gm, w3_words, w3_scales, w4_words, w4_scales, offs, hz, n1, n2, n3, n4, n5):
    xq = unpack_weight(x_words, x_scales)[:, unstriped(offs)]
    y = unpack_weight(w1_words, w1_scales).T @ xq
    top = y.max(axis=1, keepdims=True)
    ea = np.exp(f64(tau) * (y[np.arange(H)[:, None], runs(n1, H)] - top))
    z = f64(gn) * (2.0 * (y * ea))
    x_hz = unpack_weight(x_words, x_scales)[np.arange(K)[:, None], runs(hz, K)]
    d = unpack_weight(w2_words, w2_scales).T @ x_hz
    sg = sigmoid(f64(sl) * (d[:, unstriped(n2)] - f64(th)))
    st = d * sg
    z2 = f64(gm) * (st - (0.5 * st[:, unstriped(n3)]))
    h = unpack_weight(w3_words, w3_scales).T @ mxq(z, 0, "e4m3") + unpack_weight(w4_words, w4_scales).T @ mxq(z2, 0, "e4m3")
    st2 = h[np.arange(N)[:, None], runs(n4, N)] - h
    out_0 = h * (sigmoid(st2[np.arange(N)[:, None], runs(n5, N)]))
    return (out_0,) + planes(out_0)

@@ -1,0 +1,241 @@
+from contextlib import ExitStack
+
+import concourse.mybir as mybir
+
+K, T, S, N, H = 512, 2048, 256, 512, 512
+FLOPS = 4 * 2 * 512 * 512 * S
+
+F32 = mybir.dt.float32
+BF16 = mybir.dt.bfloat16
+I32 = mybir.dt.int32
+U32 = mybir.dt.uint32
+U16 = mybir.dt.uint16
+U8 = mybir.dt.uint8
+FP8X4 = mybir.dt.float8_e4m3fn_x4
+ALU = mybir.AluOpType
+ACT = mybir.ActivationFunctionType
+
+P = 128
+PACK = 4
+HALF = S // 2
+BANK = 512
+
+
+def tile_picked_hjoinepkehphopd_none_po_kernel(
+    tc, x_words, x_scales, w1_words, w1_scales, w2_words, w2_scales, tau, sl, th, gn, gm,
+    w3_words, w3_scales, w4_words, w4_scales, offs, hz, n1, n2, n3, n4, n5, out_0, out_1, out_2,
+):
+    nc = tc.nc
+    with ExitStack() as ctx:
+        sb = ctx.enter_context(tc.tile_pool(name="sb", bufs=1))
+        ps = ctx.enter_context(tc.psum_pool(name="ps", bufs=1))
+
+        def tile(name, shape, dtype, tag=""):
+            return sb.tile(shape, dtype, name=name, tag=tag or name, align_bytes=64)
+
+        def load_list(name, src):
+            dst = tile(name, [P, S // 16], U16)
+            nc.sync.dma_start(dst[:], src)
+            return dst
+
+        def load_words(queue, name, src, width):
+            dst = tile(name, [P, width], U32)
+            queue.dma_start(dst[:].bitcast(I32), src[0].rearrange("p c r -> p (c r)").bitcast(I32))
+            return dst
+
+        def load_scale_rows(queue, dst, src, first, quadrants):
+            rows = src[0].bitcast(I32)
+            for q in quadrants:
+                queue.dma_start(dst[32 * q + first : 32 * q + first + 4, :].bitcast(I32), rows[4 * q : 4 * q + 4, :])
+
+        def load_rows(queue, name, src):
+            dst = tile(name, [P, PACK], F32)
+            queue.dma_start(dst[:], src.rearrange("(p t) o -> p (t o)", t=PACK))
+            return dst
+
+        def half_cols(h):
+            return slice(h * HALF, (h + 1) * HALF)
+
+        def half_list(lst, h):
+            return lst[:, h * (HALF // 16) : (h + 1) * (HALF // 16)]
+
+        def by_fours(planes):
+            return planes.rearrange("p t (c i) -> p c t i", i=4)
+
+        def woven(dst):
+            return dst.rearrange("p (c i t) -> p c t i", i=4, t=PACK)
+
+        def product(out, w, w_scale, k, t, rhs, rhs_scale, start, stop):
+            cols = slice(t * P, (t + 1) * P)
+            nc.tensor.matmul_mx(
+                out=out, lhsT=w[:, cols].bitcast(FP8X4), lhsT_scale=w_scale[k:P, cols],
+                rhs=rhs.bitcast(FP8X4), rhs_scale=rhs_scale, start=start, stop=stop,
+            )
+
+        xs = tile("xs", [P, T], U8)
+        nc.vector.memset(xs[:, : T // 2].bitcast(I32), 0)
+        nc.gpsimd.memset(xs[:, T // 2 :].bitcast(I32), 0)
+        s1_raw = tile("s1_raw", [P, H], U8)
+        nc.vector.memset(s1_raw[:].bitcast(I32), 0)
+        s2_raw = tile("s2_raw", [P, H], U8)
+        s34_raw = tile("s34_raw", [P, N], U8)
+        zero = tile("zero", [P, 1], F32)
+
+        offs_t = load_list("offs_t", offs)
+        w1_raw = load_words(nc.scalar, "w1_raw", w1_words, H)
+        load_scale_rows(nc.sync, xs, x_scales, 0, (0, 1))
+        load_scale_rows(nc.scalar, xs, x_scales, 0, (2, 3))
+        xw = load_words(nc.sync, "xw", x_words, T)
+        load_scale_rows(nc.gpsimd, s1_raw, w1_scales, 0, (2, 3))
+        load_scale_rows(nc.scalar, s1_raw, w1_scales, 0, (0, 1))
+        tau_t = load_rows(nc.scalar, "tau_t", tau)
+        hz_t = load_list("hz_t", hz)
+        n1_t = load_list("n1_t", n1)
+        xs8 = tile("xs8", [P, T], U8)
+        nc.vector.memset(xs8[:].bitcast(I32), 0)
+        nc.gpsimd.dma_start(xs8[0:P:8, :].bitcast(I32), x_scales[0].bitcast(I32))
+        xh_s = tile("xh_s", [P, S], U8)
+        nc.vector.memset(xh_s[:].bitcast(I32), 0)
+        nc.vector.memset(s2_raw[:].bitcast(I32), 0)
+        nc.vector.memset(s34_raw[:].bitcast(I32), 0)
+        nc.vector.memset(zero[:], 0.0)
+        w2_raw = load_words(nc.sync, "w2_raw", w2_words, H)
+        load_scale_rows(nc.sync, s2_raw, w2_scales, 0, range(4))
+
+        neg_tau = tile("neg_tau", [P, PACK], F32)
+        nc.scalar.activation(neg_tau[:], tau_t[:], ACT.Copy, scale=-1.0)
+
+        xq_s = tile("xq_s", [P, S], U8)
+        nc.vector.tensor_copy(xq_s[:], xs[:].indirect(offs_t[:]))
+        s1 = tile("s1", [P, H], U8)
+        nc.gpsimd.tensor_copy(s1[:].rearrange("p (t m) -> p t m", t=PACK), s1_raw[:].rearrange("p (m t) -> p t m", t=PACK))
+        xq_w = tile("xq_w", [P, S], U32)
+        nc.vector.tensor_copy(xq_w[:], xw[:].indirect(offs_t[:]))
+        w1 = tile("w1", [P, H], U32)
+        nc.scalar.copy(w1[:].rearrange("p (t m) -> p m t", t=PACK), w1_raw[:].rearrange("p (m t) -> p m t", t=PACK))
+
+        y_ps = [ps.tile([P, BANK], F32, name=f"y_ps{t}", tag=f"bank_a{t}") for t in range(PACK)]
+        for t in range(PACK):
+            product(y_ps[t][:, :S], w1, s1, 0, t, xq_w[:], xq_s[:], True, True)
+
+        top = tile("top", [P, PACK], F32)
+        e_bias = tile("e_bias", [P, PACK], F32)
+        y = [tile(f"y{t}", [P, S], F32) for t in range(PACK)]
+        ea = [tile(f"ea{t}", [P, S], F32) for t in range(PACK)]
+        for t in range(PACK):
+            nc.vector.tensor_scalar(y[t][:], y_ps[t][:, :S], 1.0, None, ALU.mult, ALU.max, accum_out=top[:, t : t + 1])
+            nc.vector.tensor_tensor(e_bias[:, t : t + 1], top[:, t : t + 1], neg_tau[:, t : t + 1], ALU.mult)
+            for h in range(2):
+                nc.scalar.activation(
+                    ea[t][:, half_cols(h)], y[t][:].indirect(half_list(n1_t, h)), ACT.Exp,
+                    bias=e_bias[:, t : t + 1], scale=tau_t[:, t : t + 1],
+                )
+
+        xh_g = tile("xh_g", [P, S], U8)
+        nc.vector.tensor_copy(xh_g[:], xs8[:].indirect(hz_t[:]))
+        for q in range(4):
+            nc.sync.dma_start(xh_s[32 * q : 32 * q + 4, :].bitcast(I32), xh_g[32 * q : 32 * q + 32 : 8, :].bitcast(I32))
+        xh_w = tile("xh_w", [P, S], U32)
+        nc.vector.tensor_copy(xh_w[:], xw[:].indirect(hz_t[:]))
+
+        gn_t = load_rows(nc.sync, "gn_t", gn)
+        sl_t = load_rows(nc.sync, "sl_t", sl)
+        th_t = load_rows(nc.sync, "th_t", th)
+        n2_t = load_list("n2_t", n2)
+        gm_t = load_rows(nc.sync, "gm_t", gm)
+        w3_raw = load_words(nc.sync, "w3_raw", w3_words, N)
+        w4_raw = load_words(nc.sync, "w4_raw", w4_words, N)
+        load_scale_rows(nc.sync, s34_raw, w3_scales, 0, range(4))
+        load_scale_rows(nc.sync, s34_raw, w4_scales, 4, range(4))
+        n3_t = load_list("n3_t", n3)
+        n4_t = load_list("n4_t", n4)
+        n5_t = load_list("n5_t", n5)
+
+        def deal(name, raw, dtype):
+            dst = tile(name, [P, H], dtype)
+            nc.gpsimd.tensor_copy(dst[:].rearrange("p (t m) -> p t m", t=PACK), raw[:].rearrange("p (m t) -> p t m", t=PACK))
+            return dst
+
+        w2 = deal("w2", w2_raw, U32)
+        s2 = deal("s2", s2_raw, U8)
+        d_ps = [ps.tile([P, BANK], F32, name=f"d_ps{t}", tag=f"bank_b{t}") for t in range(PACK)]
+        for t in range(PACK):
+            product(d_ps[t][:, :S], w2, s2, 0, t, xh_w[:], xh_s[:], True, True)
+        w3 = deal("w3", w3_raw, U32)
+        w4 = deal("w4", w4_raw, U32)
+        s34 = deal("s34", s34_raw, U8)
+
+        gn2 = tile("gn2", [P, PACK], F32)
+        nc.vector.tensor_scalar(gn2[:], gn_t[:], 2.0, None, ALU.mult)
+        s_bias = tile("s_bias", [P, PACK], F32)
+        nc.vector.scalar_tensor_tensor(s_bias[:], sl_t[:], -1.0, th_t[:], ALU.mult, ALU.mult)
+
+        d = [tile(f"d{t}", [P, S], F32) for t in range(PACK)]
+        z_planes = tile("z_planes", [P, PACK, S], BF16)
+        for t in range(PACK):
+            nc.vector.tensor_copy(d[t][:], d_ps[t][:, :S])
+        for t in range(PACK):
+            nc.vector.scalar_tensor_tensor(z_planes[:, t, :], y_ps[t][:, :S], gn2[:, t : t + 1], ea[t][:], ALU.mult, ALU.mult)
+
+        sg = [tile(f"sg{t}", [P, S], F32) for t in range(PACK)]
+        st = tile("st", [P, PACK, S], F32)
+        for t in range(PACK):
+            for h in range(2):
+                nc.scalar.activation(
+                    sg[t][:, half_cols(h)], d[t][:].indirect(half_list(n2_t, h)), ACT.Sigmoid,
+                    bias=s_bias[:, t : t + 1], scale=sl_t[:, t : t + 1],
+                )
+
+        z_in = tile("z_in", [P, S * PACK], BF16)
+        nc.vector.tensor_copy(woven(z_in[:]), by_fours(z_planes[:]))
+        z_w = tile("z_w", [P, S], U32)
+        z_s = tile("z_s", [P, S], U8)
+        nc.vector.quantize_mx(out=z_w[:].bitcast(FP8X4), scales=z_s[:], in_=z_in[:])
+        h_ps = [ps.tile([P, BANK], F32, name=f"h_ps{t}", tag=f"bank_a{t}") for t in range(PACK)]
+        for t in range(PACK):
+            product(h_ps[t][:, :S], w3, s34, 0, t, z_w[:], z_s[:], True, False)
+
+        for t in range(PACK):
+            nc.vector.scalar_tensor_tensor(st[:, t, :], d_ps[t][:, :S], gm_t[:, t : t + 1], sg[t][:], ALU.mult, ALU.mult)
+
+        for h in range(2):
+            pulled = tile(f"pulled{h}", [P, PACK, HALF], F32)
+            for t in range(PACK):
+                nc.scalar.activation(pulled[:, t, :], st[:, t, :].indirect(half_list(n3_t, h)), ACT.Copy, scale=-0.5)
+            z2_in = tile(f"z2_in{h}", [P, HALF * PACK], BF16)
+            nc.vector.tensor_tensor(woven(z2_in[:]), by_fours(pulled[:]), by_fours(st[:, :, half_cols(h)]), ALU.add)
+            z2_w = tile(f"z2_w{h}", [P, HALF], U32)
+            z2_s = tile(f"z2_s{h}", [P, HALF], U8)
+            nc.vector.quantize_mx(out=z2_w[:].bitcast(FP8X4), scales=z2_s[:], in_=z2_in[:])
+            for t in range(PACK):
+                product(h_ps[t][:, half_cols(h)], w4, s34, 4, t, z2_w[:], z2_s[:], False, h == 1)
+
+        hh = [tile(f"hh{t}", [P, S], F32) for t in range(PACK)]
+        far = [tile(f"far{t}", [P, S], F32) for t in range(PACK)]
+        st2 = [tile(f"st2_{t}", [P, S], F32) for t in range(PACK)]
+        for t in range(PACK):
+            nc.vector.tensor_copy(hh[t][:], h_ps[t][:, :S])
+            for h in range(2):
+                nc.scalar.activation(far[t][:, half_cols(h)], hh[t][:].indirect(half_list(n4_t, h)), ACT.Copy)
+        for t in range(PACK):
+            nc.vector.tensor_tensor(st2[t][:], far[t][:], h_ps[t][:, :S], ALU.subtract)
+
+        out_rows = out_0.rearrange("(p t) j -> p t j", t=PACK)
+        out_words = out_1[0].rearrange("p c r -> p (c r)").bitcast(I32)
+        o_w = tile("o_w", [P, S], U32)
+        o_s = tile("o_s", [P, S], U8)
+        for h in range(2):
+            gate = tile(f"gate{h}", [P, PACK, HALF], F32)
+            res = tile(f"res{h}", [P, PACK, HALF], F32)
+            for t in range(PACK):
+                nc.scalar.activation(gate[:, t, :], st2[t][:].indirect(half_list(n5_t, h)), ACT.Sigmoid, bias=zero[:])
+                nc.vector.tensor_tensor(res[:, t, :], gate[:, t, :], h_ps[t][:, half_cols(h)], ALU.mult)
+            nc.sync.dma_start(out_rows[:, :, half_cols(h)], res[:])
+            o_in = tile(f"o_in{h}", [P, HALF * PACK], BF16)
+            nc.vector.tensor_copy(woven(o_in[:]), by_fours(res[:]))
+            nc.vector.quantize_mx(out=o_w[:, half_cols(h)].bitcast(FP8X4), scales=o_s[:, half_cols(h)], in_=o_in[:])
+            nc.sync.dma_start(out_words[:, half_cols(h)], o_w[:, half_cols(h)].bitcast(I32))
+        out_scale_rows = out_2[0].bitcast(I32)
+        for q in range(4):
+            queue = nc.scalar if q % 2 == 0 else nc.sync
+            queue.dma_start(out_scale_rows[4 * q : 4 * q + 4, :], o_s[32 * q : 32 * q + 4, :].bitcast(I32))

@@ -78,7 +78,7 @@ def tile_picked_hjoinepkehphopd_none_po_kernel(
         s1_raw = tile("s1_raw", [P, H], U8)
         nc.vector.memset(s1_raw[:].bitcast(I32), 0)
         s2_raw = tile("s2_raw", [P, H], U8)
-        s34_raw = tile("s34_raw", [P, N], U8)
+        s34_raw = tile("s34_raw", [P, 2 * N], U8)
         zero = tile("zero", [P, 1], F32)
 
         offs_t = load_list("offs_t", offs)
@@ -86,29 +86,49 @@ def tile_picked_hjoinepkehphopd_none_po_kernel(
         load_scale_rows(nc.sync, xs, x_scales, 0, (0, 1))
         load_scale_rows(nc.scalar, xs, x_scales, 0, (2, 3))
         xw = load_words(nc.sync, "xw", x_words, T)
-        load_scale_rows(nc.gpsimd, s1_raw, w1_scales, 0, (2, 3))
-        load_scale_rows(nc.scalar, s1_raw, w1_scales, 0, (0, 1))
+        load_scale_rows(nc.scalar, s1_raw, w1_scales, 0, range(4))
         tau_t = load_rows(nc.scalar, "tau_t", tau)
-        hz_t = load_list("hz_t", hz)
         n1_t = load_list("n1_t", n1)
+        hz_t = load_list("hz_t", hz)
         xs8 = tile("xs8", [P, T], U8)
         nc.vector.memset(xs8[:].bitcast(I32), 0)
-        nc.gpsimd.dma_start(xs8[0:P:8, :].bitcast(I32), x_scales[0].bitcast(I32))
+        nc.sync.dma_start(xs8[0:P:8, :].bitcast(I32), x_scales[0].bitcast(I32))
         xh_s = tile("xh_s", [P, S], U8)
         nc.vector.memset(xh_s[:].bitcast(I32), 0)
         nc.vector.memset(s2_raw[:].bitcast(I32), 0)
         nc.vector.memset(s34_raw[:].bitcast(I32), 0)
         nc.vector.memset(zero[:], 0.0)
-        w2_raw = load_words(nc.sync, "w2_raw", w2_words, H)
+        minus_half = tile("minus_half", [P, HALF], F32)
+        nc.vector.memset(minus_half[:], -0.5)
+        y_win = [tile(f"y_win{t}", [P, 2 * S], F32) for t in range(PACK)]
+        for t in range(PACK):
+            nc.vector.memset(y_win[t][:, S:], 0.0)
+        d_win = [tile(f"d_win{t}", [P, 2 * S], F32) for t in range(PACK)]
+        h_win = [tile(f"h_win{t}", [P, 2 * S], F32) for t in range(PACK)]
+        ea = [d_win[t][:, S:] for t in range(PACK)]
+        sg = [h_win[t][:, S:] for t in range(PACK)]
         load_scale_rows(nc.sync, s2_raw, w2_scales, 0, range(4))
+        w2_raw = load_words(nc.sync, "w2_raw", w2_words, H)
+        for a, src in enumerate((w3_scales, w4_scales)):
+            nc.sync.dma_start(s34_raw[0:16, a * N : (a + 1) * N].bitcast(I32), src[0].bitcast(I32))
+        n2_t = load_list("n2_t", n2)
+        sl_t = load_rows(nc.gpsimd, "sl_t", sl)
+        th_t = load_rows(nc.gpsimd, "th_t", th)
+        gn_t = load_rows(nc.gpsimd, "gn_t", gn)
 
+        sl_th = tile("sl_th", [P, PACK], F32)
+        nc.gpsimd.tensor_tensor(sl_th[:], sl_t[:], th_t[:], ALU.mult)
+        s_bias = tile("s_bias", [P, PACK], F32)
+        nc.gpsimd.tensor_scalar(s_bias[:], sl_th[:], -1.0, 0.0, ALU.mult, ALU.add)
+        gn2 = tile("gn2", [P, PACK], F32)
+        nc.gpsimd.tensor_scalar(gn2[:], gn_t[:], 2.0, 0.0, ALU.mult, ALU.add)
         neg_tau = tile("neg_tau", [P, PACK], F32)
         nc.scalar.activation(neg_tau[:], tau_t[:], ACT.Copy, scale=-1.0)
 
         xq_s = tile("xq_s", [P, S], U8)
         nc.vector.tensor_copy(xq_s[:], xs[:].indirect(offs_t[:]))
         s1 = tile("s1", [P, H], U8)
-        nc.gpsimd.tensor_copy(s1[:].rearrange("p (t m) -> p t m", t=PACK), s1_raw[:].rearrange("p (m t) -> p t m", t=PACK))
+        nc.vector.tensor_copy(s1[:].rearrange("p (t m) -> p m t", t=PACK), s1_raw[:].rearrange("p (m t) -> p m t", t=PACK))
         xq_w = tile("xq_w", [P, S], U32)
         nc.vector.tensor_copy(xq_w[:], xw[:].indirect(offs_t[:]))
         w1 = tile("w1", [P, H], U32)
@@ -120,71 +140,58 @@ def tile_picked_hjoinepkehphopd_none_po_kernel(
 
         top = tile("top", [P, PACK], F32)
         e_bias = tile("e_bias", [P, PACK], F32)
-        y = [tile(f"y{t}", [P, S], F32) for t in range(PACK)]
-        ea = [tile(f"ea{t}", [P, S], F32) for t in range(PACK)]
         for t in range(PACK):
-            nc.vector.tensor_scalar(y[t][:], y_ps[t][:, :S], 1.0, None, ALU.mult, ALU.max, accum_out=top[:, t : t + 1])
+            nc.vector.tensor_scalar(y_win[t][:, :S], y_ps[t][:, :S], 1.0, None, ALU.mult, ALU.max, accum_out=top[:, t : t + 1])
             nc.vector.tensor_tensor(e_bias[:, t : t + 1], top[:, t : t + 1], neg_tau[:, t : t + 1], ALU.mult)
-            for h in range(2):
-                nc.scalar.activation(
-                    ea[t][:, half_cols(h)], y[t][:].indirect(half_list(n1_t, h)), ACT.Exp,
-                    bias=e_bias[:, t : t + 1], scale=tau_t[:, t : t + 1],
-                )
+            nc.scalar.activation(
+                ea[t], y_win[t][:].indirect(n1_t[:]), ACT.Exp,
+                bias=e_bias[:, t : t + 1], scale=tau_t[:, t : t + 1],
+            )
 
         xh_g = tile("xh_g", [P, S], U8)
         nc.vector.tensor_copy(xh_g[:], xs8[:].indirect(hz_t[:]))
         for q in range(4):
             nc.sync.dma_start(xh_s[32 * q : 32 * q + 4, :].bitcast(I32), xh_g[32 * q : 32 * q + 32 : 8, :].bitcast(I32))
-        xh_w = tile("xh_w", [P, S], U32)
+        xh_w = tile("xh_w", [P, S], U32, tag="xq_w")
         nc.vector.tensor_copy(xh_w[:], xw[:].indirect(hz_t[:]))
 
-        gn_t = load_rows(nc.sync, "gn_t", gn)
-        sl_t = load_rows(nc.sync, "sl_t", sl)
-        th_t = load_rows(nc.sync, "th_t", th)
-        n2_t = load_list("n2_t", n2)
-        gm_t = load_rows(nc.sync, "gm_t", gm)
+        for q in range(1, 4):
+            nc.sync.dma_start(s34_raw[32 * q : 32 * q + 4, :].bitcast(I32), s34_raw[4 * q : 4 * q + 4, :].bitcast(I32))
         w3_raw = load_words(nc.sync, "w3_raw", w3_words, N)
         w4_raw = load_words(nc.sync, "w4_raw", w4_words, N)
-        load_scale_rows(nc.sync, s34_raw, w3_scales, 0, range(4))
-        load_scale_rows(nc.sync, s34_raw, w4_scales, 4, range(4))
+        gm_t = load_rows(nc.sync, "gm_t", gm)
         n3_t = load_list("n3_t", n3)
         n4_t = load_list("n4_t", n4)
         n5_t = load_list("n5_t", n5)
 
         def deal(name, raw, dtype):
             dst = tile(name, [P, H], dtype)
-            nc.gpsimd.tensor_copy(dst[:].rearrange("p (t m) -> p t m", t=PACK), raw[:].rearrange("p (m t) -> p t m", t=PACK))
+            nc.gpsimd.tensor_copy(dst[:].rearrange("p (t m) -> p t m", t=PACK), raw.rearrange("p (m t) -> p t m", t=PACK))
             return dst
 
-        w2 = deal("w2", w2_raw, U32)
-        s2 = deal("s2", s2_raw, U8)
+        s2 = deal("s2", s2_raw[:], U8)
+        w2 = deal("w2", w2_raw[:], U32)
         d_ps = [ps.tile([P, BANK], F32, name=f"d_ps{t}", tag=f"bank_b{t}") for t in range(PACK)]
         for t in range(PACK):
             product(d_ps[t][:, :S], w2, s2, 0, t, xh_w[:], xh_s[:], True, True)
-        w3 = deal("w3", w3_raw, U32)
-        w4 = deal("w4", w4_raw, U32)
-        s34 = deal("s34", s34_raw, U8)
+        s3 = deal("s3", s34_raw[:, :N], U8)
+        w3 = deal("w3", w3_raw[:], U32)
+        s4 = deal("s4", s34_raw[:, N:], U8)
+        w4 = deal("w4", w4_raw[:], U32)
 
-        gn2 = tile("gn2", [P, PACK], F32)
-        nc.vector.tensor_scalar(gn2[:], gn_t[:], 2.0, None, ALU.mult)
-        s_bias = tile("s_bias", [P, PACK], F32)
-        nc.vector.scalar_tensor_tensor(s_bias[:], sl_t[:], -1.0, th_t[:], ALU.mult, ALU.mult)
 
-        d = [tile(f"d{t}", [P, S], F32) for t in range(PACK)]
         z_planes = tile("z_planes", [P, PACK, S], BF16)
         for t in range(PACK):
-            nc.vector.tensor_copy(d[t][:], d_ps[t][:, :S])
+            nc.vector.tensor_copy(d_win[t][:, :S], d_ps[t][:, :S])
         for t in range(PACK):
-            nc.vector.scalar_tensor_tensor(z_planes[:, t, :], y_ps[t][:, :S], gn2[:, t : t + 1], ea[t][:], ALU.mult, ALU.mult)
+            nc.vector.scalar_tensor_tensor(z_planes[:, t, :], y_ps[t][:, :S], gn2[:, t : t + 1], ea[t], ALU.mult, ALU.mult)
 
-        sg = [tile(f"sg{t}", [P, S], F32) for t in range(PACK)]
         st = tile("st", [P, PACK, S], F32)
         for t in range(PACK):
-            for h in range(2):
-                nc.scalar.activation(
-                    sg[t][:, half_cols(h)], d[t][:].indirect(half_list(n2_t, h)), ACT.Sigmoid,
-                    bias=s_bias[:, t : t + 1], scale=sl_t[:, t : t + 1],
-                )
+            nc.scalar.activation(
+                sg[t], d_win[t][:].indirect(n2_t[:]), ACT.Sigmoid,
+                bias=s_bias[:, t : t + 1], scale=sl_t[:, t : t + 1],
+            )
 
         z_in = tile("z_in", [P, S * PACK], BF16)
         nc.vector.tensor_copy(woven(z_in[:]), by_fours(z_planes[:]))
@@ -193,14 +200,17 @@ def tile_picked_hjoinepkehphopd_none_po_kernel(
         nc.vector.quantize_mx(out=z_w[:].bitcast(FP8X4), scales=z_s[:], in_=z_in[:])
         h_ps = [ps.tile([P, BANK], F32, name=f"h_ps{t}", tag=f"bank_a{t}") for t in range(PACK)]
         for t in range(PACK):
-            product(h_ps[t][:, :S], w3, s34, 0, t, z_w[:], z_s[:], True, False)
+            product(h_ps[t][:, :S], w3, s3, 0, t, z_w[:], z_s[:], True, False)
 
         for t in range(PACK):
-            nc.vector.scalar_tensor_tensor(st[:, t, :], d_ps[t][:, :S], gm_t[:, t : t + 1], sg[t][:], ALU.mult, ALU.mult)
+            nc.vector.scalar_tensor_tensor(st[:, t, :], d_ps[t][:, :S], gm_t[:, t : t + 1], sg[t], ALU.mult, ALU.mult)
 
         for h in range(2):
             pulled = tile(f"pulled{h}", [P, PACK, HALF], F32)
-            for t in range(PACK):
+            nc.vector.tensor_tensor(
+                pulled[:, 0, :], st[:].rearrange("p t j -> p (t j)").indirect(half_list(n3_t, h)), minus_half[:], ALU.mult
+            )
+            for t in range(1, PACK):
                 nc.scalar.activation(pulled[:, t, :], st[:, t, :].indirect(half_list(n3_t, h)), ACT.Copy, scale=-0.5)
             z2_in = tile(f"z2_in{h}", [P, HALF * PACK], BF16)
             nc.vector.tensor_tensor(woven(z2_in[:]), by_fours(pulled[:]), by_fours(st[:, :, half_cols(h)]), ALU.add)
@@ -208,15 +218,13 @@ def tile_picked_hjoinepkehphopd_none_po_kernel(
             z2_s = tile(f"z2_s{h}", [P, HALF], U8)
             nc.vector.quantize_mx(out=z2_w[:].bitcast(FP8X4), scales=z2_s[:], in_=z2_in[:])
             for t in range(PACK):
-                product(h_ps[t][:, half_cols(h)], w4, s34, 4, t, z2_w[:], z2_s[:], False, h == 1)
+                product(h_ps[t][:, half_cols(h)], w4, s4, 0, t, z2_w[:], z2_s[:], False, h == 1)
 
-        hh = [tile(f"hh{t}", [P, S], F32) for t in range(PACK)]
         far = [tile(f"far{t}", [P, S], F32) for t in range(PACK)]
         st2 = [tile(f"st2_{t}", [P, S], F32) for t in range(PACK)]
         for t in range(PACK):
-            nc.vector.tensor_copy(hh[t][:], h_ps[t][:, :S])
-            for h in range(2):
-                nc.scalar.activation(far[t][:, half_cols(h)], hh[t][:].indirect(half_list(n4_t, h)), ACT.Copy)
+            nc.vector.tensor_copy(h_win[t][:, :S], h_ps[t][:, :S])
+            nc.scalar.activation(far[t][:], h_win[t][:].indirect(n4_t[:]), ACT.Copy)
         for t in range(PACK):
             nc.vector.tensor_tensor(st2[t][:], far[t][:], h_ps[t][:, :S], ALU.subtract)
 

from contextlib import ExitStack

import concourse.mybir as mybir

K, T, S, N, H = 512, 2048, 256, 512, 512
FLOPS = 4 * 2 * 512 * 512 * S

F32 = mybir.dt.float32
BF16 = mybir.dt.bfloat16
I32 = mybir.dt.int32
U32 = mybir.dt.uint32
U16 = mybir.dt.uint16
U8 = mybir.dt.uint8
FP8X4 = mybir.dt.float8_e4m3fn_x4
ALU = mybir.AluOpType
ACT = mybir.ActivationFunctionType

P = 128
PACK = 4
HALF = S // 2
BANK = 512


def tile_picked_hjoinepkehphopd_none_po_kernel(
    tc, x_words, x_scales, w1_words, w1_scales, w2_words, w2_scales, tau, sl, th, gn, gm,
    w3_words, w3_scales, w4_words, w4_scales, offs, hz, n1, n2, n3, n4, n5, out_0, out_1, out_2,
):
    nc = tc.nc
    with ExitStack() as ctx:
        sb = ctx.enter_context(tc.tile_pool(name="sb", bufs=1))
        ps = ctx.enter_context(tc.psum_pool(name="ps", bufs=1))

        def tile(name, shape, dtype, tag=""):
            return sb.tile(shape, dtype, name=name, tag=tag or name, align_bytes=64)

        def load_list(name, src):
            dst = tile(name, [P, S // 16], U16)
            nc.sync.dma_start(dst[:], src)
            return dst

        def load_words(queue, name, src, width):
            dst = tile(name, [P, width], U32)
            queue.dma_start(dst[:].bitcast(I32), src[0].rearrange("p c r -> p (c r)").bitcast(I32))
            return dst

        def load_scale_rows(queue, dst, src, first, quadrants):
            rows = src[0].bitcast(I32)
            for q in quadrants:
                queue.dma_start(dst[32 * q + first : 32 * q + first + 4, :].bitcast(I32), rows[4 * q : 4 * q + 4, :])

        def load_rows(queue, name, src):
            dst = tile(name, [P, PACK], F32)
            queue.dma_start(dst[:], src.rearrange("(p t) o -> p (t o)", t=PACK))
            return dst

        def half_cols(h):
            return slice(h * HALF, (h + 1) * HALF)

        def half_list(lst, h):
            return lst[:, h * (HALF // 16) : (h + 1) * (HALF // 16)]

        def by_fours(planes):
            return planes.rearrange("p t (c i) -> p c t i", i=4)

        def woven(dst):
            return dst.rearrange("p (c i t) -> p c t i", i=4, t=PACK)

        def product(out, w, w_scale, k, t, rhs, rhs_scale, start, stop):
            cols = slice(t * P, (t + 1) * P)
            nc.tensor.matmul_mx(
                out=out, lhsT=w[:, cols].bitcast(FP8X4), lhsT_scale=w_scale[k:P, cols],
                rhs=rhs.bitcast(FP8X4), rhs_scale=rhs_scale, start=start, stop=stop,
            )

        xs = tile("xs", [P, T], U8)
        nc.vector.memset(xs[:, : T // 2].bitcast(I32), 0)
        nc.gpsimd.memset(xs[:, T // 2 :].bitcast(I32), 0)
        s1_raw = tile("s1_raw", [P, H], U8)
        nc.vector.memset(s1_raw[:].bitcast(I32), 0)
        s2_raw = tile("s2_raw", [P, H], U8)
        s34_raw = tile("s34_raw", [P, 2 * N], U8)
        zero = tile("zero", [P, 1], F32)

        offs_t = load_list("offs_t", offs)
        w1_raw = load_words(nc.scalar, "w1_raw", w1_words, H)
        load_scale_rows(nc.sync, xs, x_scales, 0, (0, 1))
        load_scale_rows(nc.scalar, xs, x_scales, 0, (2, 3))
        xw = load_words(nc.sync, "xw", x_words, T)
        load_scale_rows(nc.scalar, s1_raw, w1_scales, 0, range(4))
        tau_t = load_rows(nc.scalar, "tau_t", tau)
        n1_t = load_list("n1_t", n1)
        hz_t = load_list("hz_t", hz)
        xs8 = tile("xs8", [P, T], U8)
        nc.vector.memset(xs8[:].bitcast(I32), 0)
        nc.sync.dma_start(xs8[0:P:8, :].bitcast(I32), x_scales[0].bitcast(I32))
        xh_s = tile("xh_s", [P, S], U8)
        nc.vector.memset(xh_s[:].bitcast(I32), 0)
        nc.vector.memset(s2_raw[:].bitcast(I32), 0)
        nc.vector.memset(s34_raw[:].bitcast(I32), 0)
        nc.vector.memset(zero[:], 0.0)
        minus_half = tile("minus_half", [P, HALF], F32)
        nc.vector.memset(minus_half[:], -0.5)
        y_win = [tile(f"y_win{t}", [P, 2 * S], F32) for t in range(PACK)]
        for t in range(PACK):
            nc.vector.memset(y_win[t][:, S:], 0.0)
        d_win = [tile(f"d_win{t}", [P, 2 * S], F32) for t in range(PACK)]
        h_win = [tile(f"h_win{t}", [P, 2 * S], F32) for t in range(PACK)]
        ea = [d_win[t][:, S:] for t in range(PACK)]
        sg = [h_win[t][:, S:] for t in range(PACK)]
        load_scale_rows(nc.sync, s2_raw, w2_scales, 0, range(4))
        w2_raw = load_words(nc.sync, "w2_raw", w2_words, H)
        for a, src in enumerate((w3_scales, w4_scales)):
            nc.sync.dma_start(s34_raw[0:16, a * N : (a + 1) * N].bitcast(I32), src[0].bitcast(I32))
        n2_t = load_list("n2_t", n2)
        sl_t = load_rows(nc.gpsimd, "sl_t", sl)
        th_t = load_rows(nc.gpsimd, "th_t", th)
        gn_t = load_rows(nc.gpsimd, "gn_t", gn)

        sl_th = tile("sl_th", [P, PACK], F32)
        nc.gpsimd.tensor_tensor(sl_th[:], sl_t[:], th_t[:], ALU.mult)
        s_bias = tile("s_bias", [P, PACK], F32)
        nc.gpsimd.tensor_scalar(s_bias[:], sl_th[:], -1.0, 0.0, ALU.mult, ALU.add)
        gn2 = tile("gn2", [P, PACK], F32)
        nc.gpsimd.tensor_scalar(gn2[:], gn_t[:], 2.0, 0.0, ALU.mult, ALU.add)
        neg_tau = tile("neg_tau", [P, PACK], F32)
        nc.scalar.activation(neg_tau[:], tau_t[:], ACT.Copy, scale=-1.0)

        xq_s = tile("xq_s", [P, S], U8)
        nc.vector.tensor_copy(xq_s[:], xs[:].indirect(offs_t[:]))
        s1 = tile("s1", [P, H], U8)
        nc.vector.tensor_copy(s1[:].rearrange("p (t m) -> p m t", t=PACK), s1_raw[:].rearrange("p (m t) -> p m t", t=PACK))
        xq_w = tile("xq_w", [P, S], U32)
        nc.vector.tensor_copy(xq_w[:], xw[:].indirect(offs_t[:]))
        w1 = tile("w1", [P, H], U32)
        nc.scalar.copy(w1[:].rearrange("p (t m) -> p m t", t=PACK), w1_raw[:].rearrange("p (m t) -> p m t", t=PACK))

        y_ps = [ps.tile([P, BANK], F32, name=f"y_ps{t}", tag=f"bank_a{t}") for t in range(PACK)]
        for t in range(PACK):
            product(y_ps[t][:, :S], w1, s1, 0, t, xq_w[:], xq_s[:], True, True)

        top = tile("top", [P, PACK], F32)
        e_bias = tile("e_bias", [P, PACK], F32)
        for t in range(PACK):
            nc.vector.tensor_scalar(y_win[t][:, :S], y_ps[t][:, :S], 1.0, None, ALU.mult, ALU.max, accum_out=top[:, t : t + 1])
            nc.vector.tensor_tensor(e_bias[:, t : t + 1], top[:, t : t + 1], neg_tau[:, t : t + 1], ALU.mult)
            nc.scalar.activation(
                ea[t], y_win[t][:].indirect(n1_t[:]), ACT.Exp,
                bias=e_bias[:, t : t + 1], scale=tau_t[:, t : t + 1],
            )

        xh_g = tile("xh_g", [P, S], U8)
        nc.vector.tensor_copy(xh_g[:], xs8[:].indirect(hz_t[:]))
        for q in range(4):
            nc.sync.dma_start(xh_s[32 * q : 32 * q + 4, :].bitcast(I32), xh_g[32 * q : 32 * q + 32 : 8, :].bitcast(I32))
        xh_w = tile("xh_w", [P, S], U32, tag="xq_w")
        nc.vector.tensor_copy(xh_w[:], xw[:].indirect(hz_t[:]))

        for q in range(1, 4):
            nc.sync.dma_start(s34_raw[32 * q : 32 * q + 4, :].bitcast(I32), s34_raw[4 * q : 4 * q + 4, :].bitcast(I32))
        w3_raw = load_words(nc.sync, "w3_raw", w3_words, N)
        w4_raw = load_words(nc.sync, "w4_raw", w4_words, N)
        gm_t = load_rows(nc.sync, "gm_t", gm)
        n3_t = load_list("n3_t", n3)
        n4_t = load_list("n4_t", n4)
        n5_t = load_list("n5_t", n5)

        def deal(name, raw, dtype):
            dst = tile(name, [P, H], dtype)
            nc.gpsimd.tensor_copy(dst[:].rearrange("p (t m) -> p t m", t=PACK), raw.rearrange("p (m t) -> p t m", t=PACK))
            return dst

        s2 = deal("s2", s2_raw[:], U8)
        w2 = deal("w2", w2_raw[:], U32)
        d_ps = [ps.tile([P, BANK], F32, name=f"d_ps{t}", tag=f"bank_b{t}") for t in range(PACK)]
        for t in range(PACK):
            product(d_ps[t][:, :S], w2, s2, 0, t, xh_w[:], xh_s[:], True, True)
        s3 = deal("s3", s34_raw[:, :N], U8)
        w3 = deal("w3", w3_raw[:], U32)
        s4 = deal("s4", s34_raw[:, N:], U8)
        w4 = deal("w4", w4_raw[:], U32)


        z_planes = tile("z_planes", [P, PACK, S], BF16)
        for t in range(PACK):
            nc.vector.tensor_copy(d_win[t][:, :S], d_ps[t][:, :S])
        for t in range(PACK):
            nc.vector.scalar_tensor_tensor(z_planes[:, t, :], y_ps[t][:, :S], gn2[:, t : t + 1], ea[t], ALU.mult, ALU.mult)

        st = tile("st", [P, PACK, S], F32)
        for t in range(PACK):
            nc.scalar.activation(
                sg[t], d_win[t][:].indirect(n2_t[:]), ACT.Sigmoid,
                bias=s_bias[:, t : t + 1], scale=sl_t[:, t : t + 1],
            )

        z_in = tile("z_in", [P, S * PACK], BF16)
        nc.vector.tensor_copy(woven(z_in[:]), by_fours(z_planes[:]))
        z_w = tile("z_w", [P, S], U32)
        z_s = tile("z_s", [P, S], U8)
        nc.vector.quantize_mx(out=z_w[:].bitcast(FP8X4), scales=z_s[:], in_=z_in[:])
        h_ps = [ps.tile([P, BANK], F32, name=f"h_ps{t}", tag=f"bank_a{t}") for t in range(PACK)]
        for t in range(PACK):
            product(h_ps[t][:, :S], w3, s3, 0, t, z_w[:], z_s[:], True, False)

        for t in range(PACK):
            nc.vector.scalar_tensor_tensor(st[:, t, :], d_ps[t][:, :S], gm_t[:, t : t + 1], sg[t], ALU.mult, ALU.mult)

        for h in range(2):
            pulled = tile(f"pulled{h}", [P, PACK, HALF], F32)
            nc.vector.tensor_tensor(
                pulled[:, 0, :], st[:].rearrange("p t j -> p (t j)").indirect(half_list(n3_t, h)), minus_half[:], ALU.mult
            )
            for t in range(1, PACK):
                nc.scalar.activation(pulled[:, t, :], st[:, t, :].indirect(half_list(n3_t, h)), ACT.Copy, scale=-0.5)
            z2_in = tile(f"z2_in{h}", [P, HALF * PACK], BF16)
            nc.vector.tensor_tensor(woven(z2_in[:]), by_fours(pulled[:]), by_fours(st[:, :, half_cols(h)]), ALU.add)
            z2_w = tile(f"z2_w{h}", [P, HALF], U32)
            z2_s = tile(f"z2_s{h}", [P, HALF], U8)
            nc.vector.quantize_mx(out=z2_w[:].bitcast(FP8X4), scales=z2_s[:], in_=z2_in[:])
            for t in range(PACK):
                product(h_ps[t][:, half_cols(h)], w4, s4, 0, t, z2_w[:], z2_s[:], False, h == 1)

        far = [tile(f"far{t}", [P, S], F32) for t in range(PACK)]
        st2 = [tile(f"st2_{t}", [P, S], F32) for t in range(PACK)]
        for t in range(PACK):
            nc.vector.tensor_copy(h_win[t][:, :S], h_ps[t][:, :S])
            nc.scalar.activation(far[t][:], h_win[t][:].indirect(n4_t[:]), ACT.Copy)
        for t in range(PACK):
            nc.vector.tensor_tensor(st2[t][:], far[t][:], h_ps[t][:, :S], ALU.subtract)

        out_rows = out_0.rearrange("(p t) j -> p t j", t=PACK)
        out_words = out_1[0].rearrange("p c r -> p (c r)").bitcast(I32)
        o_w = tile("o_w", [P, S], U32)
        o_s = tile("o_s", [P, S], U8)
        for h in range(2):
            gate = tile(f"gate{h}", [P, PACK, HALF], F32)
            res = tile(f"res{h}", [P, PACK, HALF], F32)
            for t in range(PACK):
                nc.scalar.activation(gate[:, t, :], st2[t][:].indirect(half_list(n5_t, h)), ACT.Sigmoid, bias=zero[:])
                nc.vector.tensor_tensor(res[:, t, :], gate[:, t, :], h_ps[t][:, half_cols(h)], ALU.mult)
            nc.sync.dma_start(out_rows[:, :, half_cols(h)], res[:])
            o_in = tile(f"o_in{h}", [P, HALF * PACK], BF16)
            nc.vector.tensor_copy(woven(o_in[:]), by_fours(res[:]))
            nc.vector.quantize_mx(out=o_w[:, half_cols(h)].bitcast(FP8X4), scales=o_s[:, half_cols(h)], in_=o_in[:])
            nc.sync.dma_start(out_words[:, half_cols(h)], o_w[:, half_cols(h)].bitcast(I32))
        out_scale_rows = out_2[0].bitcast(I32)
        for q in range(4):
            queue = nc.scalar if q % 2 == 0 else nc.sync
            queue.dma_start(out_scale_rows[4 * q : 4 * q + 4, :], o_s[32 * q : 32 * q + 4, :].bitcast(I32))
